import numpy as np, ml_dtypes
CORES = [40,64,80,88,96,104,120,144]
N = 8
import mx_ref
BF = ml_dtypes.bfloat16
def entries(a):
    return np.ascontiguousarray(a.T).reshape(-1)
def table(e):
    return np.ascontiguousarray(np.reshape(e, (-1, 16)).T).astype(np.int32)
def cols(t, e):
    v = np.concatenate([t.reshape(128, -1, 4), np.zeros((128, 1, 4), BF)], axis=1)
    return np.ascontiguousarray(v[:, e]).reshape(128, -1)
def f(rng, *shape):
    return mx_ref.flush((rng.standard_normal(shape, dtype=np.float32) * np.exp2(rng.integers(-2, 3, shape[:-1] + (1,)))).astype(BF))
def wide(rng, *shape, cols=0):
    v = rng.standard_normal(shape, dtype=np.float32) * np.exp2(rng.integers(-12, 13, shape)).astype(np.float32)
    if cols: v *= np.repeat(np.exp2(rng.integers(-cols, cols + 1, shape[:-2] + (1, shape[-1] // 4))) * (rng.random(shape[:-2] + (1, shape[-1] // 4)) > 0.0625), 4, axis=-1).astype(np.float32)
    return mx_ref.flush(v.astype(BF))
T, CAPP = 256, 48
def lists(rng, full=False, skew=False, single=False, back=False):
    if full:
        v = rng.permutation(([CAPP] * (T // CAPP) + [T % CAPP] + [0] * N)[:N])
        n = v[(np.arange(N)[None, :] - np.arange(N)[:, None]) % N][rng.permutation(N)][:, rng.permutation(N)]
    else:
        n = np.full((N, N), T // N)
        for _ in range(20 * N):
            (s, t), (d, e) = rng.permutation(N)[:2], rng.permutation(N)[:2]
            k = rng.integers(0, min(n[s, d], n[t, e], CAPP - n[s, e], CAPP - n[t, d]) + 1)
            n[s, d] -= k; n[t, e] -= k; n[s, e] += k; n[t, d] += k
    a = np.full((N, N * CAPP), -1)
    for s in range(N):
        parts = np.split(rng.permutation(T), np.cumsum(n[s])[:-1])
        for d in range(N): a[s, d * CAPP + rng.permutation(CAPP)[:n[s, d]]] = parts[d]
    p, u, o = [], [], []
    for r in range(N):
        used = np.flatnonzero(a[:, r * CAPP:(r + 1) * CAPP].reshape(-1) >= 0)
        p.append(table(used[::-1] if back else rng.permutation(used)))
        h = rng.integers(0, N)
        c = rng.integers(0, 2, N) if full else (np.full(N, -1) if rng.random() < 0.5 else rng.integers(0, 2, N)) if single else rng.integers(-1, 2, N)
        if c[h] < 0: c[h] = rng.integers(0, 2)
        named = np.flatnonzero(c >= 0)
        if single: named = np.array([h])
        if skew:
            m = rng.integers(T // 2 + 1, T + 1)
            e = np.sort(np.concatenate([np.full(m, h), rng.choice(named, T - m)]))
        elif full: e = np.sort(np.concatenate([named, rng.choice(named, T - N)]))
        else: e = np.repeat(named, np.diff(np.concatenate([[0], np.sort(rng.integers(0, T + 1, len(named) - 1)), [T]])))
        u.append(table(np.concatenate([c, np.full(16 - N, -1)]))); o.append(table(e))
    return {"send": np.stack([table(k) for k in a]), "place": np.stack(p), "sel": np.stack(u), "of": np.stack(o)}
def setup_inputs(rng):
    return {"x": f(rng, N, 128, 4 * T), "w": f(rng, N, 256, 512), **lists(rng)}
def setup_inputs_full(rng):
    return {**setup_inputs(rng), **lists(rng, full=True)}
def setup_inputs_reversed(rng):
    return {**setup_inputs(rng), **lists(rng, back=True)}
def setup_inputs_single(rng):
    return {**setup_inputs(rng), **lists(rng, single=True)}
def setup_inputs_skew(rng):
    return {**setup_inputs(rng), **lists(rng, skew=True)}
def setup_inputs_spread(rng):
    d = setup_inputs(rng); d["x"] = wide(rng, N, 128, 4 * T, cols=8); return d
def check_inputs(d):
    b = []
    for k in ("x", "w"):
        a = np.abs(d[k].astype(np.float32))
        if not ((a == 0) | ((a >= 2.0 ** -30) & (a <= 2.0 ** 30))).all(): b.append(k)
    sends = np.stack([entries(d["send"][r]) for r in range(N)])
    for r in range(N):
        c, p, u, e = sends[r], entries(d["place"][r]), entries(d["sel"][r]), entries(d["of"][r])
        if c.min() < -1 or not np.array_equal(np.sort(c[c >= 0]), np.arange(T)): b.append("send")
        if not np.array_equal(np.sort(p), np.flatnonzero(sends[:, r * CAPP:(r + 1) * CAPP].reshape(-1) >= 0)): b.append("place")
        if u.min() < -1 or u.max() > 1 or (u[N:] != -1).any(): b.append("sel")
        if e.min() < 0 or e.max() >= N or (np.diff(e) < 0).any() or (u[e] < 0).any(): b.append("of")
    return b
def reference(x, w, send, place, sel, of):
    W = [[mx_ref.quantize(w[h][128 * m:128 * m + 128]) for m in range(2)] for h in range(N)]
    y = np.zeros((N, 128, T), np.float32)
    for r in range(N):
        slots = np.concatenate([cols(x[s], entries(send[s])[r * CAPP:(r + 1) * CAPP]) for s in range(N)], axis=1)
        X = mx_ref.quantize(cols(slots, entries(place[r])))
        u, e = entries(sel[r]), entries(of[r])
        for h in range(N):
            i = e == h
            if i.any(): y[r][:, i] = mx_ref.matmul(W[h][u[h]], X)[:, i]
    return {"y": y}

@@ -1,0 +1,423 @@
+from concourse.bass import DstId, RemoteDMATransfer
+from concourse.mybir import dt, AluOpType, ActivationFunctionType
+
+N, COLS, CAPP, ROWS = 8, 256, 48, 128
+SL = N * CAPP
+NEAR0, FAR0, OWN0 = 0, 4, 8
+SEL_ENGS = 4
+
+SCRATCH = {
+    "selsrc": ("dram", [128, 1], "int32"),
+    "rsel": ("dram", [128, 1], "int32"),
+    "selin": ("dram", [N, 128, 1], "int32"),
+    "selt": ("sbuf", [128, 12], "int32"),
+    "selo": ("sbuf", [128, 12], "uint16"),
+    "two": ("sbuf", [128, 2], "float32"),
+    "bc": ("sbuf", [128, 16 * 12], "float32"),
+    "ip": ("sbuf", [128, 32], "int32"),
+    "ic": ("sbuf", [128, 32], "int32"),
+    "pm": ("sbuf", [128, 32], "int32"),
+    "base": ("sbuf", [128, 32], "int32"),
+    "woff": ("sbuf", [128, 32 * N], "uint16"),
+    "sendr": ("sbuf", [128, SL // 16], "int32"),
+    "xoff": ("sbuf", [128, SL // 16], "uint16"),
+    "xb": ("sbuf", [128, 4 * COLS], "bfloat16"),
+    "xs": ("sbuf", [128, 4 * SL], "bfloat16"),
+    "xq": ("sbuf", [128, SL], "float8_e4m3fn_x4"),
+    "xp": ("sbuf", [128, SL], "uint8"),
+    "xc": ("sbuf", [128, SL], "float8_e4m3fn_x4"),
+    "xcp": ("sbuf", [128, SL], "uint8"),
+    "wb": ("sbuf", [128, 1024], "bfloat16"),
+    "ws": ("sbuf", [128, 512 * N], "bfloat16"),
+    "wq": ("sbuf", [128, ROWS * N], "float8_e4m3fn_x4"),
+    "wp": ("sbuf", [128, ROWS * N], "uint8"),
+    "ec": ("sbuf", [128, ROWS * N], "float8_e4m3fn_x4"),
+    "ep": ("sbuf", [128, ROWS * N], "uint8"),
+    "rc": ("sbuf", [128, CAPP], "float8_e4m3fn_x4"),
+    "rcp": ("sbuf", [128, CAPP], "uint8"),
+    "rt": ("sbuf", [128, ROWS], "float8_e4m3fn_x4"),
+    "rtp": ("sbuf", [128, ROWS], "uint8"),
+    "ht": ("sbuf", [128, ROWS], "float8_e4m3fn_x4"),
+    "htp": ("sbuf", [128, ROWS], "uint8"),
+    "plr": ("sbuf", [16, 16], "int32"),
+    "ofr": ("sbuf", [16, 16], "int32"),
+    "ofm": ("sbuf", [16, 16], "int32"),
+    "ysum": ("sbuf", [16, 16], "int32"),
+    "y16": ("sbuf", [16, 16], "uint16"),
+    "yoff": ("sbuf", [128, 16], "uint16"),
+    "res": ("sbuf", [128, SL * N], "float32"),
+    "yo": ("sbuf", [128, COLS], "float32"),
+    "ps": ("psum", [128, 512 * N], "float32"),
+}
+SEMAPHORES = (["lsel", "lown", "lnear", "lsend", "lx", "lw", "lpo", "lyo", "own", "it", "two", "vb", "vx", "xg",
+               "xgs", "xqd", "vown", "von", "voa", "vga", "sga0", "sga1", "sgo", "hq", "aq", "oq", "vp1", "vp2", "vp3",
+               "vbf", "vob0", "vob1", "vb0", "sb0", "bq0", "vb1", "sb1", "bq1", "sela", "selx", "cx", "c0", "cv", "cs",
+               "yv", "ys", "stv", "sts", "ls", "rcc", "rcp", "rtc", "rtp", "htc", "htp"]
+              + ["e%d" % h for h in range(N)] + ["m%d" % h for h in range(N)])
+
+
+def near_ranks(topo, cores, r):
+    return [d % N for d in range(r + 1, r + N) if topo.may_write(cores[r], cores[d % N])]
+
+
+def far_ranks(topo, cores, r):
+    return [d for d in range(N) if d != r and not topo.may_write(cores[r], cores[d])]
+
+
+def relays(topo, cores, r):
+    far = far_ranks(topo, cores, r)
+    c = [k for k in topo.cores_of(cores[r]) if k != cores[r] and all(topo.may_write(k, cores[d]) for d in far)]
+    a = [k for k in c if topo.die(k) != topo.die(cores[r])]
+    b = [k for k in c if topo.die(k) == topo.die(cores[r])]
+    return [k for pair in zip(a, b) for k in pair]
+
+
+def helper(topo, cores, r):
+    return relays(topo, cores, r)[2]
+
+
+def slot(topo, cores, s, d):
+    i = sorted([s] + near_ranks(topo, cores, s)).index(s)
+    j = sorted([d] + near_ranks(topo, cores, d)).index(d)
+    return (i + j) % len(relays(topo, cores, s))
+
+
+def far_sorted(topo, cores, r):
+    return sorted(far_ranks(topo, cores, r), key=lambda d: slot(topo, cores, r, d))
+
+
+def bits(engs):
+    return sum(1 << e for e in engs)
+
+
+def lace(engs, parts):
+    n = 2 * len(engs) // parts
+    out = []
+    for k in range(parts // 2):
+        out += [engs[k * n:(k + 1) * n:2], engs[k * n + 1:(k + 1) * n:2]]
+    return out
+
+
+def outer(topo, cores, s):
+    return topo.engines(cores[s], cores[near_ranks(topo, cores, s)[0]])
+
+
+def inner(topo, cores, s):
+    return [e for e in topo.engines(cores[s], helper(topo, cores, s)) if e not in outer(topo, cores, s)]
+
+
+def near_col_engs(topo, cores, s, d, plane):
+    e = outer(topo, cores, s)
+    h, q = len(e) // 2, len(e) // 4
+    e = e[h:] + e[:h] if plane else e
+    return [e[:h], e[h:h + q], e[h + q:]][near_ranks(topo, cores, s).index(d)]
+
+
+def far_col_engs(topo, cores, s, k):
+    return lace(inner(topo, cores, s), len(relays(topo, cores, s)))[k]
+
+
+def near_tile_engs(topo, cores, s, d):
+    return inner(topo, cores, s) if d == near_ranks(topo, cores, s)[0] else outer(topo, cores, s)
+
+
+def far_tile_engs(topo, cores, s, k):
+    return lace(topo.engines(cores[s], relays(topo, cores, s)[k]), 2)[k % 2]
+
+
+def landed(topo, cores, s, r, experts):
+    if r in near_ranks(topo, cores, s):
+        if not experts:
+            return sum(len(near_col_engs(topo, cores, s, r, p)) for p in (0, 1))
+        if r != near_ranks(topo, cores, s)[0]:
+            return 2 * len(near_tile_engs(topo, cores, s, r))
+        c = helper(topo, cores, s)
+    else:
+        c = relays(topo, cores, s)[slot(topo, cores, s, r)]
+    return 2 * len(topo.engines(c, cores[r]))
+
+
+def u8(v):
+    return v.bitcast(dt.uint8)
+
+
+def cut(h, n):
+    return slice(h * n, (h + 1) * n)
+
+
+def dst_id(topo, core, dst):
+    rid, pid = topo.addr(dst, core)
+    return DstId(rid=rid, pnc=pid)
+
+
+def xfer(topo, core, dst, engs, sem, src, out):
+    return RemoteDMATransfer(dst_ids=[dst_id(topo, core, dst)], dma_engine_mask=bits(engs), remote_sem=sem,
+                             srcs=[src], dsts=[out])
+
+
+def rank_program(g, core, T, topo):
+    cores = list(T.cores)
+    r = T.rank_of(core)
+    if r is not None:
+        rank_core(g, core, T, topo, cores, r)
+        return
+    for s in range(N):
+        if core in relays(topo, cores, s):
+            relay_core(g, core, T, topo, cores, s)
+
+
+def relay_core(g, core, T, topo, cores, s):
+    S = T.sem
+    k = relays(topo, cores, s).index(core)
+    d = far_sorted(topo, cores, s)[k]
+    e = topo.engines(core, cores[d])
+    sent = [0]
+
+    def on(sem, n, to, engs, rsem, out, src):
+        g.wait_ge(sem, n)
+        rid, pid = topo.addr(cores[to], core)
+        g.remote_dma(out, src, rsem, S.ls, pid, rid, bits(engs))
+        sent[0] += len(engs)
+
+    c = FAR0 + far_ranks(topo, cores, d).index(s)
+    on(S.sela, 1, d, e[:SEL_ENGS], S.selx, T.selt[:, c:c + 1], T.rsel[:])
+    n = len(far_col_engs(topo, cores, s, k))
+    on(S.rcc, n, d, e, S.cx, u8(T.xc[:, cut(s, CAPP)]), u8(T.rc[:]))
+    on(S.rcp, n, d, e, S.cx, T.xcp[:, cut(s, CAPP)], T.rcp[:])
+    if core == helper(topo, cores, s):
+        h = near_ranks(topo, cores, s)[0]
+        eh = topo.engines(core, cores[h])
+        n = len(near_tile_engs(topo, cores, s, h))
+        on(S.htc, n, h, eh, S["e%d" % s], u8(T.ec[:, cut(s, ROWS)]), u8(T.ht[:]))
+        on(S.htp, n, h, eh, S["e%d" % s], T.ep[:, cut(s, ROWS)], T.htp[:])
+    n = len(far_tile_engs(topo, cores, s, k))
+    on(S.rtc, n, d, e, S["e%d" % s], u8(T.ec[:, cut(s, ROWS)]), u8(T.rt[:]))
+    on(S.rtp, n, d, e, S["e%d" % s], T.ep[:, cut(s, ROWS)], T.rtp[:])
+    g.wait_ge(S.ls, sent[0])
+
+
+def rank_core(g, core, T, topo, cores, r):
+    S = T.sem
+    near, far, rel = near_ranks(topo, cores, r), far_sorted(topo, cores, r), relays(topo, cores, r)
+    hlp = helper(topo, cores, r)
+    V, A, P, Y = g.vector, g.scalar, g.tensor, g.sync
+    Copy = ActivationFunctionType.Copy
+    add, mult, big = AluOpType.add, AluOpType.mult, AluOpType.max
+
+    def ofs(d):
+        return T.woff[:, cut(d, 32)]
+
+    def expert(d):
+        return T.wb[:].indirect(ofs(d))
+
+    def made(d):
+        return T.ws[:, cut(d, 512)]
+
+    def quantise(d, sem):
+        V.quantize_mx(T.wq[:, cut(d, ROWS)], T.wp[:, cut(d, ROWS)], made(d)).then_inc(sem, 1)
+
+    order = [r] + near + sorted(far, key=lambda h: slot(topo, cores, h, r))
+    last, half = order[-1], SL // 2
+
+    for q in range(0, 4):
+        Y.dma_start(T.selsrc[cut(q, 16), :], T.sel[:]).then_inc(S.lsel, 16)
+    for q in range(0, 4):
+        Y.dma_start(T.sendr[cut(q, 16), :], T.send[:]).then_inc(S.lsend, 16)
+    for m in range(2):
+        Y.dma_start(T.wb[:, cut(m, 512)], T.w[cut(m, 128), :]).then_inc(S.lw, 16)
+    Y.wait_ge(S.lsel, 128)
+    Y.dma_start(T.selt[:, OWN0:OWN0 + 1], T.selsrc[:]).then_inc(S.lown, 16)
+    Y.dma_start(T.plr[:], T.place[:]).then_inc(S.lpo, 16)
+    Y.dma_start(T.ofr[:], T.of[:]).then_inc(S.lpo, 16)
+    Y.wait_ge(S.xqd, 1)
+    Y.dma_start(u8(T.xc[:, cut(r, CAPP)]), u8(T.xq[:, cut(r, CAPP)])).then_inc(S.own, 16)
+    Y.dma_start(T.xcp[:, cut(r, CAPP)], T.xp[:, cut(r, CAPP)]).then_inc(S.own, 16)
+    Y.wait_ge(S.sela, len(near))
+    for i, d in enumerate(near):
+        Y.dma_start(T.selt[:, NEAR0 + i:NEAR0 + i + 1], T.selin[d]).then_inc(S.lnear, 16)
+    Y.wait_ge(S.vp3, 1)
+    for q in range(8):
+        Y.dma_start(T.yoff[cut(q, 16), :], T.y16[:]).then_inc(S.lyo, 16)
+    Y.wait_ge(S.yv, 1)
+    Y.dma_start(T.y[:, 0:128], T.yo[:, 0:128]).then_inc(S.stv, 16)
+    Y.wait_ge(S.stv, 16)
+
+    g.iota(T.ip[:], [[0, 32]], 0, 1).then_inc(S.it, 1)
+    g.iota(T.ic[:], [[16, 32]], 0, 0).then_inc(S.it, 1)
+    g.wait_ge(S.lsel, 128)
+    g.remote_dma_fused([RemoteDMATransfer(
+        dst_ids=[dst_id(topo, core, c) for c in rel + [cores[d] for d in near]],
+        dma_engine_mask=bits(outer(topo, cores, r)[:1]), remote_sem=S.sela,
+        srcs=[T.selsrc[:]], dsts=[T.rsel[:] for c in rel] + [T.selin[r] for d in near])], local_sem=S.ls)
+    sent = 1
+
+    g.wait_ge(S.xqd, 1)
+    for plane, src, via, to, sem in (
+            (0, lambda d: u8(T.xq[:, cut(d, CAPP)]), u8(T.rc[:]), u8(T.xc[:, cut(r, CAPP)]), S.rcc),
+            (1, lambda d: T.xp[:, cut(d, CAPP)], T.rcp[:], T.xcp[:, cut(r, CAPP)], S.rcp)):
+        ts = []
+        for k, d in enumerate(far):
+            e = far_col_engs(topo, cores, r, k)
+            ts.append(xfer(topo, core, rel[k], e, sem, src(d), via))
+            sent += len(e)
+        for d in near:
+            e = near_col_engs(topo, cores, r, d, plane)
+            ts.append(xfer(topo, core, cores[d], e, S.cx, src(d), to))
+            sent += len(e)
+        g.remote_dma_fused(ts, local_sem=S.ls)
+
+    def tiles(dests):
+        n = 0
+        for src, via, to, sem, hvia, hsem in (
+                (lambda d: u8(T.wq[:, cut(d, ROWS)]), u8(T.rt[:]), u8(T.ec[:, cut(r, ROWS)]), S.rtc, u8(T.ht[:]), S.htc),
+                (lambda d: T.wp[:, cut(d, ROWS)], T.rtp[:], T.ep[:, cut(r, ROWS)], S.rtp, T.htp[:], S.htp)):
+            ts = []
+            for d in dests:
+                if d in far:
+                    k = far.index(d)
+                    e = far_tile_engs(topo, cores, r, k)
+                    ts.append(xfer(topo, core, rel[k], e, sem, src(d), via))
+                else:
+                    e = near_tile_engs(topo, cores, r, d)
+                    ts.append(xfer(topo, core, hlp, e, hsem, src(d), hvia) if d == near[0] else
+                              xfer(topo, core, cores[d], e, S["e%d" % r], src(d), to))
+                n += len(e)
+            g.remote_dma_fused(ts, local_sem=S.ls)
+        return n
+
+    g.wait_ge(S.hq, 2)
+    sent += tiles(near[:2])
+    g.wait_ge(S.aq, 1)
+    sent += tiles(near[2:])
+    for b in range(2):
+        g.wait_ge(S["bq%d" % b], 2)
+        sent += tiles(far[2 * b:2 * b + 2])
+    g.wait_ge(S.ls, sent)
+
+    def spread(c, n, sem):
+        V.tensor_copy(T.selo[:, c:c + n], T.selt[:, c:c + n]).then_inc(sem, 1)
+        V.wait_ge(sem, 1)
+        V.tensor_copy(T.bc[:, 16 * c:16 * (c + n)], T.two[:].indirect(T.selo[:, c:c + n])).then_inc(sem, 1)
+        V.wait_ge(sem, 2)
+
+    def aim(d, c, sem):
+        V.tensor_scalar(ofs(d), T.base[:], T.bc[:, 16 * c + r:16 * c + r + 1], None, add).then_inc(sem, 1)
+
+    V.memset(T.two[:, 0:1], 0.0).then_inc(S.two, 1)
+    V.memset(T.two[:, 1:2], 512.0).then_inc(S.two, 1)
+    V.wait_ge(S.it, 2)
+    V.tensor_scalar(T.pm[:], T.ip[:], 15, None, AluOpType.bitwise_and).then_inc(S.vb, 1)
+    V.wait_ge(S.vb, 1)
+    V.tensor_tensor(T.base[:], T.pm[:], T.ic[:], add).then_inc(S.vb, 1)
+    V.wait_ge(S.lsend, 128)
+    V.tensor_scalar(T.xoff[:], T.sendr[:], 0.0, 4.0, big, mult).then_inc(S.vx, 1)
+    V.wait_ge(S.vx, 1)
+    V.wait_ge(S.lx, 16)
+    for t in (0, 1):
+        V.tensor_copy(T.xs[:, t:4 * SL:4], T.xb[:, t:4 * COLS].indirect(T.xoff[:])).then_inc(S.xg, 1)
+    V.wait_ge(S.xg, 2)
+    V.wait_ge(S.xgs, 2)
+    V.quantize_mx(T.xq[:], T.xp[:], T.xs[:]).then_inc(S.xqd, 1)
+    V.wait_ge(S.vb, 2)
+    V.wait_ge(S.two, 2)
+    V.wait_ge(S.lown, 16)
+    spread(OWN0, 1, S.vown)
+    aim(r, OWN0, S.vown)
+    V.wait_ge(S.lpo, 32)
+    V.tensor_scalar(T.ofm[:], T.ofr[:], float(SL), None, mult).then_inc(S.vp1, 1)
+    V.wait_ge(S.vp1, 1)
+    V.tensor_tensor(T.ysum[:], T.ofm[:], T.plr[:], add).then_inc(S.vp2, 1)
+    V.wait_ge(S.vp2, 1)
+    V.tensor_copy(T.y16[:], T.ysum[:]).then_inc(S.vp3, 1)
+    V.wait_ge(S.lnear, 16 * len(near))
+    spread(NEAR0, len(near), S.von)
+    for i, d in enumerate(near):
+        aim(d, NEAR0 + i, S.voa)
+    V.wait_ge(S.voa, len(near))
+    V.wait_ge(S.lw, 32)
+    V.tensor_copy(made(near[0]), expert(near[0])).then_inc(S.vga, 1)
+    V.wait_ge(S.vga, 1)
+    quantise(near[0], S.hq)
+    V.wait_ge(S.sgo, 1)
+    V.quantize_mx(T.ec[:, cut(r, ROWS)], T.ep[:, cut(r, ROWS)], made(r)).then_inc(S.oq, 1)
+    V.wait_ge(S.sga0, 1)
+    quantise(near[1], S.hq)
+    fcol = far_ranks(topo, cores, r)
+    V.wait_ge(S.selx, SEL_ENGS * len(far))
+    spread(FAR0, len(far), S.vbf)
+    for d in far[:2]:
+        aim(d, FAR0 + fcol.index(d), S.vob0)
+    V.wait_ge(S.vob0, 2)
+    for b in range(2):
+        d, c = far[2 * b], far[2 * b + 1]
+        V.tensor_copy(made(d), expert(d)).then_inc(S["vb%d" % b], 1)
+        if b == 0:
+            for d2 in far[2:]:
+                aim(d2, FAR0 + fcol.index(d2), S.vob1)
+            V.wait_ge(S.sga1, 1)
+            quantise(near[2], S.aq)
+        V.wait_ge(S["vb%d" % b], 1)
+        quantise(d, S["bq%d" % b])
+        V.wait_ge(S["sb%d" % b], 1)
+        quantise(c, S["bq%d" % b])
+        if b == 0:
+            V.wait_ge(S.vob1, 2)
+    V.wait_ge(S.m0, 1)
+    V.tensor_copy(T.res[:, cut(r, SL)], T.ps[:, 512 * r:512 * r + SL]).then_inc(S.c0, 1)
+    for i, h in enumerate(order[:-1]):
+        if i and i % 2 == 0:
+            V.wait_ge(S["m%d" % i], 1)
+            V.tensor_copy(T.res[:, cut(h, SL)], T.ps[:, 512 * h:512 * h + SL]).then_inc(S.cv, 1)
+    V.wait_ge(S.m7, 2)
+    V.tensor_copy(T.res[:, SL * last:SL * last + half], T.ps[:, 512 * last:512 * last + half]).then_inc(S.cv, 1)
+    V.wait_ge(S.lyo, 128)
+    V.wait_ge(S.c0, 1)
+    V.wait_ge(S.cv, 4)
+    V.wait_ge(S.cs, 4)
+    V.tensor_copy(T.yo[:, 0:128], T.res[:].indirect(T.yoff[:, 0:8])).then_inc(S.yv, 1)
+
+    for q in range(4, 8):
+        A.dma_start(T.selsrc[cut(q, 16), :], T.sel[:]).then_inc(S.lsel, 16)
+    for q in range(4, 8):
+        A.dma_start(T.sendr[cut(q, 16), :], T.send[:]).then_inc(S.lsend, 16)
+    A.dma_start(T.xb[:], T.x[:]).then_inc(S.lx, 16)
+    A.wait_ge(S.vx, 1)
+    A.wait_ge(S.lx, 16)
+    for t in (2, 3):
+        A.activation(T.xs[:, t:4 * SL:4], T.xb[:, t:4 * COLS].indirect(T.xoff[:]), Copy).then_inc(S.xgs, 1)
+    A.wait_ge(S.lw, 32)
+    A.wait_ge(S.vown, 3)
+    A.activation(made(r), expert(r), Copy).then_inc(S.sgo, 1)
+    A.wait_ge(S.voa, len(near))
+    for i, d in enumerate(near[1:]):
+        A.activation(made(d), expert(d), Copy).then_inc(S["sga%d" % i], 1)
+    for b in range(2):
+        A.wait_ge(S["vob%d" % b], 2)
+        d = far[2 * b + 1]
+        A.activation(made(d), expert(d), Copy).then_inc(S["sb%d" % b], 1)
+    for i, h in enumerate(order[:-1]):
+        if i % 2 == 1:
+            A.wait_ge(S["m%d" % i], 1)
+            A.activation(T.res[:, cut(h, SL)], T.ps[:, 512 * h:512 * h + SL], Copy).then_inc(S.cs, 1)
+    A.wait_ge(S.m7, 2)
+    A.activation(T.res[:, SL * last + half:SL * (last + 1)], T.ps[:, 512 * r:512 * r + half], Copy).then_inc(S.cs, 1)
+    A.wait_ge(S.lyo, 128)
+    A.wait_ge(S.cs, 4)
+    A.wait_ge(S.c0, 1)
+    A.wait_ge(S.cv, 4)
+    A.activation(T.yo[:, 128:256], T.res[:].indirect(T.yoff[:, 8:16]), Copy).then_inc(S.ys, 1)
+    A.wait_ge(S.ys, 1)
+    A.dma_start(T.y[:, 128:256], T.yo[:, 128:256]).then_inc(S.sts, 16)
+    A.wait_ge(S.sts, 16)
+
+    P.wait_ge(S.own, 32)
+    P.wait_ge(S.cx, sum(landed(topo, cores, s, r, False) for s in near + far))
+    for i, h in enumerate(order):
+        w, p = T.ec[:, cut(h, ROWS)], T.ep[:, cut(h, ROWS)]
+        P.wait_ge(S.oq if h == r else S["e%d" % h], 1 if h == r else landed(topo, cores, h, r, True))
+        if h != last:
+            P.matmul_mx(T.ps[:, 512 * h:512 * h + SL], w, p, T.xc[:], T.xcp[:], True, True).then_inc(S["m%d" % i], 1)
+        else:
+            P.wait_ge(S.c0, 1)
+            P.matmul_mx(T.ps[:, 512 * h:512 * h + half], w, p, T.xc[:, 0:half], T.xcp[:, 0:half], True, True).then_inc(S.m7, 1)
+            P.matmul_mx(T.ps[:, 512 * r:512 * r + half], w, p, T.xc[:, half:SL], T.xcp[:, half:SL], True, True).then_inc(S.m7, 1)

@@ -4,12 +4,14 @@ from concourse.mybir import dt, AluOpType, ActivationFunctionType
 N, COLS, CAPP, ROWS = 8, 256, 48, 128
 SL = N * CAPP
 NEAR0, FAR0, OWN0 = 0, 4, 8
-SEL_ENGS = 4
+VPART = 8
+HLP = 2
+BOTH = 3
+NEAR_ENGS, SEL_ENGS = 2, 4
 
 SCRATCH = {
     "selsrc": ("dram", [128, 1], "int32"),
     "rsel": ("dram", [128, 1], "int32"),
-    "selin": ("dram", [N, 128, 1], "int32"),
     "selt": ("sbuf", [128, 12], "int32"),
     "selo": ("sbuf", [128, 12], "uint16"),
     "two": ("sbuf", [128, 2], "float32"),
@@ -35,25 +37,36 @@ SCRATCH = {
     "ep": ("sbuf", [128, ROWS * N], "uint8"),
     "rc": ("sbuf", [128, CAPP], "float8_e4m3fn_x4"),
     "rcp": ("sbuf", [128, CAPP], "uint8"),
+    "rc2": ("sbuf", [128, CAPP], "float8_e4m3fn_x4"),
+    "rcp2": ("sbuf", [128, CAPP], "uint8"),
     "rt": ("sbuf", [128, ROWS], "float8_e4m3fn_x4"),
     "rtp": ("sbuf", [128, ROWS], "uint8"),
+    "uq": ("sbuf", [128, 2 * ROWS], "float8_e4m3fn_x4"),
+    "up": ("sbuf", [128, 2 * ROWS], "uint8"),
+    "ru": ("sbuf", [128, 2 * ROWS], "float8_e4m3fn_x4"),
+    "rup": ("sbuf", [128, 2 * ROWS], "uint8"),
+    "eu": ("sbuf", [128, 2 * ROWS], "float8_e4m3fn_x4"),
+    "eup": ("sbuf", [128, 2 * ROWS], "uint8"),
     "ht": ("sbuf", [128, ROWS], "float8_e4m3fn_x4"),
     "htp": ("sbuf", [128, ROWS], "uint8"),
     "plr": ("sbuf", [16, 16], "int32"),
     "ofr": ("sbuf", [16, 16], "int32"),
     "ofm": ("sbuf", [16, 16], "int32"),
     "ysum": ("sbuf", [16, 16], "int32"),
+    "ofu": ("sbuf", [16, 16], "int32"),
+    "ofv": ("sbuf", [16, 16], "int32"),
+    "yall": ("sbuf", [16, 16], "int32"),
     "y16": ("sbuf", [16, 16], "uint16"),
     "yoff": ("sbuf", [128, 16], "uint16"),
-    "res": ("sbuf", [128, SL * N], "float32"),
+    "res": ("sbuf", [128, SL * (N + 1)], "float32"),
     "yo": ("sbuf", [128, COLS], "float32"),
     "ps": ("psum", [128, 512 * N], "float32"),
 }
-SEMAPHORES = (["lsel", "lown", "lnear", "lsend", "lx", "lw", "lpo", "lyo", "own", "it", "two", "vb", "vx", "xg",
-               "xgs", "xqd", "vown", "von", "voa", "vga", "sga0", "sga1", "sgo", "hq", "aq", "oq", "vp1", "vp2", "vp3",
-               "vbf", "vob0", "vob1", "vb0", "sb0", "bq0", "vb1", "sb1", "bq1", "sela", "selx", "cx", "c0", "cv", "cs",
-               "yv", "ys", "stv", "sts", "ls", "rcc", "rcp", "rtc", "rtp", "htc", "htp"]
-              + ["e%d" % h for h in range(N)] + ["m%d" % h for h in range(N)])
+SEMAPHORES = (["lsel", "lown", "lsend", "lx", "lw", "lpo", "lyo", "own", "it", "two", "vb", "vx", "xg",
+               "xgs", "xqd", "uqd", "vown", "von", "voa", "vga", "sga0", "sga1", "sgo", "hq", "oq", "vp1", "vp2", "vp3", "vp4",
+               "vbf", "vob0", "vob1", "vb0", "sb0", "bq0", "vb1", "sb1", "bq1", "sela", "seln", "selx", "cx", "c0", "c1",
+               "cv", "cs", "yv", "ys", "stv", "sts", "ls", "rcc", "rcp", "rtc", "rtp", "htc", "htp", "ruc", "rup"]
+              + ["e%d" % h for h in range(N)] + ["m%d" % h for h in range(N + 1)])
 
 
 def near_ranks(topo, cores, r):
@@ -69,11 +82,11 @@ def relays(topo, cores, r):
     c = [k for k in topo.cores_of(cores[r]) if k != cores[r] and all(topo.may_write(k, cores[d]) for d in far)]
     a = [k for k in c if topo.die(k) != topo.die(cores[r])]
     b = [k for k in c if topo.die(k) == topo.die(cores[r])]
-    return [k for pair in zip(a, b) for k in pair]
+    return [b[0], a[0], b[1], a[0]]
 
 
 def helper(topo, cores, r):
-    return relays(topo, cores, r)[2]
+    return relays(topo, cores, r)[HLP]
 
 
 def slot(topo, cores, s, d):
@@ -122,7 +135,8 @@ def near_tile_engs(topo, cores, s, d):
 
 
 def far_tile_engs(topo, cores, s, k):
-    return lace(topo.engines(cores[s], relays(topo, cores, s)[k]), 2)[k % 2]
+    e = topo.engines(cores[s], relays(topo, cores, s)[k])
+    return lace(e, 2)[k] if k < 2 else inner(topo, cores, s) if k == 2 else e
 
 
 def landed(topo, cores, s, r, experts):
@@ -134,6 +148,8 @@ def landed(topo, cores, s, r, experts):
         c = helper(topo, cores, s)
     else:
         c = relays(topo, cores, s)[slot(topo, cores, s, r)]
+        if not experts:
+            return 2 * len(topo.engines(c, cores[r])) // relays(topo, cores, s).count(c)
     return 2 * len(topo.engines(c, cores[r]))
 
 
@@ -168,31 +184,41 @@ def rank_program(g, core, T, topo):
 
 def relay_core(g, core, T, topo, cores, s):
     S = T.sem
-    k = relays(topo, cores, s).index(core)
-    d = far_sorted(topo, cores, s)[k]
+    rel, far = relays(topo, cores, s), far_sorted(topo, cores, s)
+    ks = [k for k in range(len(rel)) if rel[k] == core]
+    k, d = ks[0], far[ks[0]]
     e = topo.engines(core, cores[d])
     sent = [0]
 
-    def on(sem, n, to, engs, rsem, out, src):
+    def on(sem, n, to, rsem, out, src, engs=e):
         g.wait_ge(sem, n)
         rid, pid = topo.addr(cores[to], core)
         g.remote_dma(out, src, rsem, S.ls, pid, rid, bits(engs))
         sent[0] += len(engs)
 
-    c = FAR0 + far_ranks(topo, cores, d).index(s)
-    on(S.sela, 1, d, e[:SEL_ENGS], S.selx, T.selt[:, c:c + 1], T.rsel[:])
-    n = len(far_col_engs(topo, cores, s, k))
-    on(S.rcc, n, d, e, S.cx, u8(T.xc[:, cut(s, CAPP)]), u8(T.rc[:]))
-    on(S.rcp, n, d, e, S.cx, T.xcp[:, cut(s, CAPP)], T.rcp[:])
+    on(S.sela, 1, d, S.selx, T.selt[:, FAR0 + k:FAR0 + k + 1], T.rsel[:], e[:SEL_ENGS])
+    n = sum(len(far_col_engs(topo, cores, s, k)) for k in ks)
+    for sem, out, srcs in ((S.rcc, u8(T.xc[:, cut(s, CAPP)]), (u8(T.rc[:]), u8(T.rc2[:]))),
+                           (S.rcp, T.xcp[:, cut(s, CAPP)], (T.rcp[:], T.rcp2[:]))):
+        if len(ks) == 1:
+            on(sem, n, d, S.cx, out, srcs[0])
+        else:
+            g.wait_ge(sem, n)
+            g.remote_dma_fused([xfer(topo, core, cores[far[q]], lace(e, 2)[i], S.cx, srcs[i], out)
+                                for i, q in enumerate(ks)], local_sem=S.ls)
+            sent[0] += len(e)
     if core == helper(topo, cores, s):
         h = near_ranks(topo, cores, s)[0]
-        eh = topo.engines(core, cores[h])
         n = len(near_tile_engs(topo, cores, s, h))
-        on(S.htc, n, h, eh, S["e%d" % s], u8(T.ec[:, cut(s, ROWS)]), u8(T.ht[:]))
-        on(S.htp, n, h, eh, S["e%d" % s], T.ep[:, cut(s, ROWS)], T.htp[:])
+        on(S.htc, n, h, S["e%d" % s], u8(T.ec[:, cut(s, ROWS)]), u8(T.ht[:]))
+        on(S.htp, n, h, S["e%d" % s], T.ep[:, cut(s, ROWS)], T.htp[:])
+    if BOTH in ks:
+        n = len(far_tile_engs(topo, cores, s, BOTH))
+        on(S.ruc, n, far[BOTH], S["e%d" % s], u8(T.eu[:]), u8(T.ru[:]))
+        on(S.rup, n, far[BOTH], S["e%d" % s], T.eup[:], T.rup[:])
     n = len(far_tile_engs(topo, cores, s, k))
-    on(S.rtc, n, d, e, S["e%d" % s], u8(T.ec[:, cut(s, ROWS)]), u8(T.rt[:]))
-    on(S.rtp, n, d, e, S["e%d" % s], T.ep[:, cut(s, ROWS)], T.rtp[:])
+    on(S.rtc, n, d, S["e%d" % s], u8(T.ec[:, cut(s, ROWS)]), u8(T.rt[:]))
+    on(S.rtp, n, d, S["e%d" % s], T.ep[:, cut(s, ROWS)], T.rtp[:])
     g.wait_ge(S.ls, sent[0])
 
 
@@ -213,10 +239,16 @@ def rank_core(g, core, T, topo, cores, r):
     def made(d):
         return T.ws[:, cut(d, 512)]
 
+    def part(d, q):
+        a, b = (0, VPART) if q == 0 else (VPART, 32)
+        return T.ws[:, 512 * d + 16 * a:512 * d + 16 * b], T.wb[:].indirect(T.woff[:, 32 * d + a:32 * d + b])
+
     def quantise(d, sem):
         V.quantize_mx(T.wq[:, cut(d, ROWS)], T.wp[:, cut(d, ROWS)], made(d)).then_inc(sem, 1)
 
-    order = [r] + near + sorted(far, key=lambda h: slot(topo, cores, h, r))
+    by_slot = sorted(far, key=lambda h: slot(topo, cores, h, r))
+    both = by_slot[BOTH]
+    order = [r, near[1], both, N, near[2], near[0]] + by_slot[:BOTH]
     last, half = order[-1], SL // 2
 
     for q in range(0, 4):
@@ -232,9 +264,6 @@ def rank_core(g, core, T, topo, cores, r):
     Y.wait_ge(S.xqd, 1)
     Y.dma_start(u8(T.xc[:, cut(r, CAPP)]), u8(T.xq[:, cut(r, CAPP)])).then_inc(S.own, 16)
     Y.dma_start(T.xcp[:, cut(r, CAPP)], T.xp[:, cut(r, CAPP)]).then_inc(S.own, 16)
-    Y.wait_ge(S.sela, len(near))
-    for i, d in enumerate(near):
-        Y.dma_start(T.selt[:, NEAR0 + i:NEAR0 + i + 1], T.selin[d]).then_inc(S.lnear, 16)
     Y.wait_ge(S.vp3, 1)
     for q in range(8):
         Y.dma_start(T.yoff[cut(q, 16), :], T.y16[:]).then_inc(S.lyo, 16)
@@ -246,25 +275,37 @@ def rank_core(g, core, T, topo, cores, r):
     g.iota(T.ic[:], [[16, 32]], 0, 0).then_inc(S.it, 1)
     g.wait_ge(S.lsel, 128)
     g.remote_dma_fused([RemoteDMATransfer(
-        dst_ids=[dst_id(topo, core, c) for c in rel + [cores[d] for d in near]],
-        dma_engine_mask=bits(outer(topo, cores, r)[:1]), remote_sem=S.sela,
-        srcs=[T.selsrc[:]], dsts=[T.rsel[:] for c in rel] + [T.selin[r] for d in near])], local_sem=S.ls)
+        dst_ids=[dst_id(topo, core, c) for c in rel[:BOTH]], dma_engine_mask=bits(outer(topo, cores, r)[:1]),
+        remote_sem=S.sela, srcs=[T.selsrc[:]], dsts=[T.rsel[:] for c in rel[:BOTH]])], local_sem=S.ls)
     sent = 1
+    ts = []
+    for k, d in enumerate(near):
+        c = NEAR0 + near_ranks(topo, cores, d).index(r)
+        e = outer(topo, cores, r)[k * NEAR_ENGS:(k + 1) * NEAR_ENGS]
+        ts.append(xfer(topo, core, cores[d], e, S.seln, T.selsrc[:], T.selt[:, c:c + 1]))
+        sent += len(e)
+    g.remote_dma_fused(ts, local_sem=S.ls)
 
     g.wait_ge(S.xqd, 1)
-    for plane, src, via, to, sem in (
-            (0, lambda d: u8(T.xq[:, cut(d, CAPP)]), u8(T.rc[:]), u8(T.xc[:, cut(r, CAPP)]), S.rcc),
-            (1, lambda d: T.xp[:, cut(d, CAPP)], T.rcp[:], T.xcp[:, cut(r, CAPP)], S.rcp)):
+    for plane, src, via, via2, to, sem in (
+            (0, lambda d: u8(T.xq[:, cut(d, CAPP)]), u8(T.rc[:]), u8(T.rc2[:]), u8(T.xc[:, cut(r, CAPP)]), S.rcc),
+            (1, lambda d: T.xp[:, cut(d, CAPP)], T.rcp[:], T.rcp2[:], T.xcp[:, cut(r, CAPP)], S.rcp)):
         ts = []
         for k, d in enumerate(far):
             e = far_col_engs(topo, cores, r, k)
-            ts.append(xfer(topo, core, rel[k], e, sem, src(d), via))
+            ts.append(xfer(topo, core, rel[k], e, sem, src(d), via2 if k == BOTH else via))
             sent += len(e)
         for d in near:
             e = near_col_engs(topo, cores, r, d, plane)
             ts.append(xfer(topo, core, cores[d], e, S.cx, src(d), to))
             sent += len(e)
         g.remote_dma_fused(ts, local_sem=S.ls)
+    g.wait_ge(S.uqd, 1)
+    e = far_tile_engs(topo, cores, r, BOTH)
+    for src, via, sem in ((u8(T.uq[:]), u8(T.ru[:]), S.ruc), (T.up[:], T.rup[:], S.rup)):
+        rid, pid = topo.addr(rel[BOTH], core)
+        g.remote_dma(via, src, sem, S.ls, pid, rid, bits(e))
+        sent += len(e)
 
     def tiles(dests):
         n = 0
@@ -287,11 +328,10 @@ def rank_core(g, core, T, topo, cores, r):
 
     g.wait_ge(S.hq, 2)
     sent += tiles(near[:2])
-    g.wait_ge(S.aq, 1)
-    sent += tiles(near[2:])
-    for b in range(2):
-        g.wait_ge(S["bq%d" % b], 2)
-        sent += tiles(far[2 * b:2 * b + 2])
+    g.wait_ge(S.bq0, 2)
+    sent += tiles(far[:2])
+    g.wait_ge(S.bq1, 2)
+    sent += tiles(near[2:] + far[2:3])
     g.wait_ge(S.ls, sent)
 
     def spread(c, n, sem):
@@ -315,6 +355,8 @@ def rank_core(g, core, T, topo, cores, r):
     V.wait_ge(S.lx, 16)
     for t in (0, 1):
         V.tensor_copy(T.xs[:, t:4 * SL:4], T.xb[:, t:4 * COLS].indirect(T.xoff[:])).then_inc(S.xg, 1)
+    V.wait_ge(S.lw, 32)
+    V.quantize_mx(T.uq[:], T.up[:], T.wb[:]).then_inc(S.uqd, 1)
     V.wait_ge(S.xg, 2)
     V.wait_ge(S.xgs, 2)
     V.quantize_mx(T.xq[:], T.xp[:], T.xs[:]).then_inc(S.xqd, 1)
@@ -324,17 +366,21 @@ def rank_core(g, core, T, topo, cores, r):
     spread(OWN0, 1, S.vown)
     aim(r, OWN0, S.vown)
     V.wait_ge(S.lpo, 32)
+    c = 16 * OWN0 + both
     V.tensor_scalar(T.ofm[:], T.ofr[:], float(SL), None, mult).then_inc(S.vp1, 1)
-    V.wait_ge(S.vp1, 1)
+    V.tensor_scalar(T.ofu[:], T.ofr[:], float(both), T.bc[0:16, c:c + 1], AluOpType.is_equal, mult).then_inc(S.vp1, 1)
+    V.wait_ge(S.vp1, 2)
     V.tensor_tensor(T.ysum[:], T.ofm[:], T.plr[:], add).then_inc(S.vp2, 1)
-    V.wait_ge(S.vp2, 1)
-    V.tensor_copy(T.y16[:], T.ysum[:]).then_inc(S.vp3, 1)
-    V.wait_ge(S.lnear, 16 * len(near))
+    V.tensor_scalar(T.ofv[:], T.ofu[:], (N - both) * SL / 512.0, None, mult).then_inc(S.vp2, 1)
+    V.wait_ge(S.vp2, 2)
+    V.tensor_tensor(T.yall[:], T.ysum[:], T.ofv[:], add).then_inc(S.vp4, 1)
+    V.wait_ge(S.vp4, 1)
+    V.tensor_copy(T.y16[:], T.yall[:]).then_inc(S.vp3, 1)
+    V.wait_ge(S.seln, NEAR_ENGS * len(near))
     spread(NEAR0, len(near), S.von)
     for i, d in enumerate(near):
         aim(d, NEAR0 + i, S.voa)
     V.wait_ge(S.voa, len(near))
-    V.wait_ge(S.lw, 32)
     V.tensor_copy(made(near[0]), expert(near[0])).then_inc(S.vga, 1)
     V.wait_ge(S.vga, 1)
     quantise(near[0], S.hq)
@@ -342,36 +388,39 @@ def rank_core(g, core, T, topo, cores, r):
     V.quantize_mx(T.ec[:, cut(r, ROWS)], T.ep[:, cut(r, ROWS)], made(r)).then_inc(S.oq, 1)
     V.wait_ge(S.sga0, 1)
     quantise(near[1], S.hq)
-    fcol = far_ranks(topo, cores, r)
-    V.wait_ge(S.selx, SEL_ENGS * len(far))
-    spread(FAR0, len(far), S.vbf)
+    V.wait_ge(S.selx, SEL_ENGS * BOTH)
+    spread(FAR0, BOTH, S.vbf)
     for d in far[:2]:
-        aim(d, FAR0 + fcol.index(d), S.vob0)
+        aim(d, FAR0 + far.index(d), S.vob0)
     V.wait_ge(S.vob0, 2)
-    for b in range(2):
-        d, c = far[2 * b], far[2 * b + 1]
-        V.tensor_copy(made(d), expert(d)).then_inc(S["vb%d" % b], 1)
-        if b == 0:
-            for d2 in far[2:]:
-                aim(d2, FAR0 + fcol.index(d2), S.vob1)
-            V.wait_ge(S.sga1, 1)
-            quantise(near[2], S.aq)
-        V.wait_ge(S["vb%d" % b], 1)
-        quantise(d, S["bq%d" % b])
-        V.wait_ge(S["sb%d" % b], 1)
-        quantise(c, S["bq%d" % b])
-        if b == 0:
-            V.wait_ge(S.vob1, 2)
-    V.wait_ge(S.m0, 1)
-    V.tensor_copy(T.res[:, cut(r, SL)], T.ps[:, 512 * r:512 * r + SL]).then_inc(S.c0, 1)
-    for i, h in enumerate(order[:-1]):
-        if i and i % 2 == 0:
-            V.wait_ge(S["m%d" % i], 1)
-            V.tensor_copy(T.res[:, cut(h, SL)], T.ps[:, 512 * h:512 * h + SL]).then_inc(S.cv, 1)
-    V.wait_ge(S.m7, 2)
-    V.tensor_copy(T.res[:, SL * last:SL * last + half], T.ps[:, 512 * last:512 * last + half]).then_inc(S.cv, 1)
+    V.tensor_copy(made(far[0]), expert(far[0])).then_inc(S.vb0, 1)
+    aim(far[2], FAR0 + 2, S.vob1)
+    V.wait_ge(S.vb0, 1)
+    quantise(far[0], S.bq0)
+    V.wait_ge(S.sb0, 1)
+    quantise(far[1], S.bq0)
+    V.wait_ge(S.vob1, 1)
+    V.tensor_copy(*part(far[2], 0)).then_inc(S.vb1, 1)
+    V.wait_ge(S.sga1, 1)
+    quantise(near[2], S.bq1)
+    V.wait_ge(S.vb1, 1)
+    V.wait_ge(S.sb1, 1)
+    quantise(far[2], S.bq1)
+
+    def bank(i):
+        return 512 * i
+
+    def block(i):
+        return cut(order[i], SL)
+
+    for i in range(0, N, 2):
+        V.wait_ge(S["m%d" % i], 1)
+        V.tensor_copy(T.res[:, block(i)], T.ps[:, bank(i):bank(i) + SL]).then_inc(S.c0 if i == 0 else S.cv, 1)
+    V.wait_ge(S.m8, 2)
+    V.tensor_copy(T.res[:, SL * last:SL * last + half], T.ps[:, 0:half]).then_inc(S.cv, 1)
     V.wait_ge(S.lyo, 128)
     V.wait_ge(S.c0, 1)
+    V.wait_ge(S.c1, 1)
     V.wait_ge(S.cv, 4)
     V.wait_ge(S.cs, 4)
     V.tensor_copy(T.yo[:, 0:128], T.res[:].indirect(T.yoff[:, 0:8])).then_inc(S.yv, 1)
@@ -391,18 +440,18 @@ def rank_core(g, core, T, topo, cores, r):
     A.wait_ge(S.voa, len(near))
     for i, d in enumerate(near[1:]):
         A.activation(made(d), expert(d), Copy).then_inc(S["sga%d" % i], 1)
-    for b in range(2):
-        A.wait_ge(S["vob%d" % b], 2)
-        d = far[2 * b + 1]
-        A.activation(made(d), expert(d), Copy).then_inc(S["sb%d" % b], 1)
-    for i, h in enumerate(order[:-1]):
-        if i % 2 == 1:
-            A.wait_ge(S["m%d" % i], 1)
-            A.activation(T.res[:, cut(h, SL)], T.ps[:, 512 * h:512 * h + SL], Copy).then_inc(S.cs, 1)
-    A.wait_ge(S.m7, 2)
-    A.activation(T.res[:, SL * last + half:SL * (last + 1)], T.ps[:, 512 * r:512 * r + half], Copy).then_inc(S.cs, 1)
+    A.wait_ge(S.vob0, 2)
+    A.activation(made(far[1]), expert(far[1]), Copy).then_inc(S.sb0, 1)
+    A.wait_ge(S.vob1, 1)
+    A.activation(*part(far[2], 1), Copy).then_inc(S.sb1, 1)
+    for i in range(1, N, 2):
+        A.wait_ge(S["m%d" % i], 1)
+        A.activation(T.res[:, block(i)], T.ps[:, bank(i):bank(i) + SL], Copy).then_inc(S.c1 if i == 1 else S.cs, 1)
+    A.wait_ge(S.m8, 2)
+    A.activation(T.res[:, SL * last + half:SL * (last + 1)], T.ps[:, 512:512 + half], Copy).then_inc(S.cs, 1)
     A.wait_ge(S.lyo, 128)
     A.wait_ge(S.cs, 4)
+    A.wait_ge(S.c1, 1)
     A.wait_ge(S.c0, 1)
     A.wait_ge(S.cv, 4)
     A.activation(T.yo[:, 128:256], T.res[:].indirect(T.yoff[:, 8:16]), Copy).then_inc(S.ys, 1)
@@ -413,11 +462,17 @@ def rank_core(g, core, T, topo, cores, r):
     P.wait_ge(S.own, 32)
     P.wait_ge(S.cx, sum(landed(topo, cores, s, r, False) for s in near + far))
     for i, h in enumerate(order):
-        w, p = T.ec[:, cut(h, ROWS)], T.ep[:, cut(h, ROWS)]
-        P.wait_ge(S.oq if h == r else S["e%d" % h], 1 if h == r else landed(topo, cores, h, r, True))
-        if h != last:
-            P.matmul_mx(T.ps[:, 512 * h:512 * h + SL], w, p, T.xc[:], T.xcp[:], True, True).then_inc(S["m%d" % i], 1)
+        if h in (both, N):
+            m = int(h == N)
+            w, p = T.eu[:, cut(m, ROWS)], T.eup[:, cut(m, ROWS)]
+            P.wait_ge(S["e%d" % both], landed(topo, cores, both, r, True))
+        else:
+            w, p = T.ec[:, cut(h, ROWS)], T.ep[:, cut(h, ROWS)]
+            P.wait_ge(S.oq if h == r else S["e%d" % h], 1 if h == r else landed(topo, cores, h, r, True))
+        if i < N:
+            P.matmul_mx(T.ps[:, bank(i):bank(i) + SL], w, p, T.xc[:], T.xcp[:], True, True).then_inc(S["m%d" % i], 1)
         else:
             P.wait_ge(S.c0, 1)
-            P.matmul_mx(T.ps[:, 512 * h:512 * h + half], w, p, T.xc[:, 0:half], T.xcp[:, 0:half], True, True).then_inc(S.m7, 1)
-            P.matmul_mx(T.ps[:, 512 * r:512 * r + half], w, p, T.xc[:, half:SL], T.xcp[:, half:SL], True, True).then_inc(S.m7, 1)
+            P.matmul_mx(T.ps[:, 0:half], w, p, T.xc[:, 0:half], T.xcp[:, 0:half], True, True).then_inc(S.m8, 1)
+            P.wait_ge(S.c1, 1)
+            P.matmul_mx(T.ps[:, 512:512 + half], w, p, T.xc[:, half:SL], T.xcp[:, half:SL], True, True).then_inc(S.m8, 1)

from concourse.bass import DstId, RemoteDMATransfer
from concourse.mybir import dt, AluOpType, ActivationFunctionType

N, COLS, CAPP, ROWS = 8, 256, 48, 128
SL = N * CAPP
NEAR0, FAR0, OWN0 = 0, 4, 8
VPART = 8
HLP = 2
BOTH = 3
NEAR_ENGS, SEL_ENGS = 2, 4

SCRATCH = {
    "selsrc": ("dram", [128, 1], "int32"),
    "rsel": ("dram", [128, 1], "int32"),
    "selt": ("sbuf", [128, 12], "int32"),
    "selo": ("sbuf", [128, 12], "uint16"),
    "two": ("sbuf", [128, 2], "float32"),
    "bc": ("sbuf", [128, 16 * 12], "float32"),
    "ip": ("sbuf", [128, 32], "int32"),
    "ic": ("sbuf", [128, 32], "int32"),
    "pm": ("sbuf", [128, 32], "int32"),
    "base": ("sbuf", [128, 32], "int32"),
    "woff": ("sbuf", [128, 32 * N], "uint16"),
    "sendr": ("sbuf", [128, SL // 16], "int32"),
    "xoff": ("sbuf", [128, SL // 16], "uint16"),
    "xb": ("sbuf", [128, 4 * COLS], "bfloat16"),
    "xs": ("sbuf", [128, 4 * SL], "bfloat16"),
    "xq": ("sbuf", [128, SL], "float8_e4m3fn_x4"),
    "xp": ("sbuf", [128, SL], "uint8"),
    "xc": ("sbuf", [128, SL], "float8_e4m3fn_x4"),
    "xcp": ("sbuf", [128, SL], "uint8"),
    "wb": ("sbuf", [128, 1024], "bfloat16"),
    "ws": ("sbuf", [128, 512 * N], "bfloat16"),
    "wq": ("sbuf", [128, ROWS * N], "float8_e4m3fn_x4"),
    "wp": ("sbuf", [128, ROWS * N], "uint8"),
    "ec": ("sbuf", [128, ROWS * N], "float8_e4m3fn_x4"),
    "ep": ("sbuf", [128, ROWS * N], "uint8"),
    "rc": ("sbuf", [128, CAPP], "float8_e4m3fn_x4"),
    "rcp": ("sbuf", [128, CAPP], "uint8"),
    "rc2": ("sbuf", [128, CAPP], "float8_e4m3fn_x4"),
    "rcp2": ("sbuf", [128, CAPP], "uint8"),
    "rt": ("sbuf", [128, ROWS], "float8_e4m3fn_x4"),
    "rtp": ("sbuf", [128, ROWS], "uint8"),
    "uq": ("sbuf", [128, 2 * ROWS], "float8_e4m3fn_x4"),
    "up": ("sbuf", [128, 2 * ROWS], "uint8"),
    "ru": ("sbuf", [128, 2 * ROWS], "float8_e4m3fn_x4"),
    "rup": ("sbuf", [128, 2 * ROWS], "uint8"),
    "eu": ("sbuf", [128, 2 * ROWS], "float8_e4m3fn_x4"),
    "eup": ("sbuf", [128, 2 * ROWS], "uint8"),
    "ht": ("sbuf", [128, ROWS], "float8_e4m3fn_x4"),
    "htp": ("sbuf", [128, ROWS], "uint8"),
    "plr": ("sbuf", [16, 16], "int32"),
    "ofr": ("sbuf", [16, 16], "int32"),
    "ofm": ("sbuf", [16, 16], "int32"),
    "ysum": ("sbuf", [16, 16], "int32"),
    "ofu": ("sbuf", [16, 16], "int32"),
    "ofv": ("sbuf", [16, 16], "int32"),
    "yall": ("sbuf", [16, 16], "int32"),
    "y16": ("sbuf", [16, 16], "uint16"),
    "yoff": ("sbuf", [128, 16], "uint16"),
    "res": ("sbuf", [128, SL * (N + 1)], "float32"),
    "yo": ("sbuf", [128, COLS], "float32"),
    "ps": ("psum", [128, 512 * N], "float32"),
}
SEMAPHORES = (["lsel", "lown", "lsend", "lx", "lw", "lpo", "lyo", "own", "it", "two", "vb", "vx", "xg",
               "xgs", "xqd", "uqd", "vown", "von", "voa", "vga", "sga0", "sga1", "sgo", "hq", "oq", "vp1", "vp2", "vp3", "vp4",
               "vbf", "vob0", "vob1", "vb0", "sb0", "bq0", "vb1", "sb1", "bq1", "sela", "seln", "selx", "cx", "c0", "c1",
               "cv", "cs", "yv", "ys", "stv", "sts", "ls", "rcc", "rcp", "rtc", "rtp", "htc", "htp", "ruc", "rup"]
              + ["e%d" % h for h in range(N)] + ["m%d" % h for h in range(N + 1)])


def near_ranks(topo, cores, r):
    return [d % N for d in range(r + 1, r + N) if topo.may_write(cores[r], cores[d % N])]


def far_ranks(topo, cores, r):
    return [d for d in range(N) if d != r and not topo.may_write(cores[r], cores[d])]


def relays(topo, cores, r):
    far = far_ranks(topo, cores, r)
    c = [k for k in topo.cores_of(cores[r]) if k != cores[r] and all(topo.may_write(k, cores[d]) for d in far)]
    a = [k for k in c if topo.die(k) != topo.die(cores[r])]
    b = [k for k in c if topo.die(k) == topo.die(cores[r])]
    return [b[0], a[0], b[1], a[0]]


def helper(topo, cores, r):
    return relays(topo, cores, r)[HLP]


def slot(topo, cores, s, d):
    i = sorted([s] + near_ranks(topo, cores, s)).index(s)
    j = sorted([d] + near_ranks(topo, cores, d)).index(d)
    return (i + j) % len(relays(topo, cores, s))


def far_sorted(topo, cores, r):
    return sorted(far_ranks(topo, cores, r), key=lambda d: slot(topo, cores, r, d))


def bits(engs):
    return sum(1 << e for e in engs)


def lace(engs, parts):
    n = 2 * len(engs) // parts
    out = []
    for k in range(parts // 2):
        out += [engs[k * n:(k + 1) * n:2], engs[k * n + 1:(k + 1) * n:2]]
    return out


def outer(topo, cores, s):
    return topo.engines(cores[s], cores[near_ranks(topo, cores, s)[0]])


def inner(topo, cores, s):
    return [e for e in topo.engines(cores[s], helper(topo, cores, s)) if e not in outer(topo, cores, s)]


def near_col_engs(topo, cores, s, d, plane):
    e = outer(topo, cores, s)
    h, q = len(e) // 2, len(e) // 4
    e = e[h:] + e[:h] if plane else e
    return [e[:h], e[h:h + q], e[h + q:]][near_ranks(topo, cores, s).index(d)]


def far_col_engs(topo, cores, s, k):
    return lace(inner(topo, cores, s), len(relays(topo, cores, s)))[k]


def near_tile_engs(topo, cores, s, d):
    return inner(topo, cores, s) if d == near_ranks(topo, cores, s)[0] else outer(topo, cores, s)


def far_tile_engs(topo, cores, s, k):
    e = topo.engines(cores[s], relays(topo, cores, s)[k])
    return lace(e, 2)[k] if k < 2 else inner(topo, cores, s) if k == 2 else e


def landed(topo, cores, s, r, experts):
    if r in near_ranks(topo, cores, s):
        if not experts:
            return sum(len(near_col_engs(topo, cores, s, r, p)) for p in (0, 1))
        if r != near_ranks(topo, cores, s)[0]:
            return 2 * len(near_tile_engs(topo, cores, s, r))
        c = helper(topo, cores, s)
    else:
        c = relays(topo, cores, s)[slot(topo, cores, s, r)]
        if not experts:
            return 2 * len(topo.engines(c, cores[r])) // relays(topo, cores, s).count(c)
    return 2 * len(topo.engines(c, cores[r]))


def u8(v):
    return v.bitcast(dt.uint8)


def cut(h, n):
    return slice(h * n, (h + 1) * n)


def dst_id(topo, core, dst):
    rid, pid = topo.addr(dst, core)
    return DstId(rid=rid, pnc=pid)


def xfer(topo, core, dst, engs, sem, src, out):
    return RemoteDMATransfer(dst_ids=[dst_id(topo, core, dst)], dma_engine_mask=bits(engs), remote_sem=sem,
                             srcs=[src], dsts=[out])


def rank_program(g, core, T, topo):
    cores = list(T.cores)
    r = T.rank_of(core)
    if r is not None:
        rank_core(g, core, T, topo, cores, r)
        return
    for s in range(N):
        if core in relays(topo, cores, s):
            relay_core(g, core, T, topo, cores, s)


def relay_core(g, core, T, topo, cores, s):
    S = T.sem
    rel, far = relays(topo, cores, s), far_sorted(topo, cores, s)
    ks = [k for k in range(len(rel)) if rel[k] == core]
    k, d = ks[0], far[ks[0]]
    e = topo.engines(core, cores[d])
    sent = [0]

    def on(sem, n, to, rsem, out, src, engs=e):
        g.wait_ge(sem, n)
        rid, pid = topo.addr(cores[to], core)
        g.remote_dma(out, src, rsem, S.ls, pid, rid, bits(engs))
        sent[0] += len(engs)

    on(S.sela, 1, d, S.selx, T.selt[:, FAR0 + k:FAR0 + k + 1], T.rsel[:], e[:SEL_ENGS])
    n = sum(len(far_col_engs(topo, cores, s, k)) for k in ks)
    for sem, out, srcs in ((S.rcc, u8(T.xc[:, cut(s, CAPP)]), (u8(T.rc[:]), u8(T.rc2[:]))),
                           (S.rcp, T.xcp[:, cut(s, CAPP)], (T.rcp[:], T.rcp2[:]))):
        if len(ks) == 1:
            on(sem, n, d, S.cx, out, srcs[0])
        else:
            g.wait_ge(sem, n)
            g.remote_dma_fused([xfer(topo, core, cores[far[q]], lace(e, 2)[i], S.cx, srcs[i], out)
                                for i, q in enumerate(ks)], local_sem=S.ls)
            sent[0] += len(e)
    if core == helper(topo, cores, s):
        h = near_ranks(topo, cores, s)[0]
        n = len(near_tile_engs(topo, cores, s, h))
        on(S.htc, n, h, S["e%d" % s], u8(T.ec[:, cut(s, ROWS)]), u8(T.ht[:]))
        on(S.htp, n, h, S["e%d" % s], T.ep[:, cut(s, ROWS)], T.htp[:])
    if BOTH in ks:
        n = len(far_tile_engs(topo, cores, s, BOTH))
        on(S.ruc, n, far[BOTH], S["e%d" % s], u8(T.eu[:]), u8(T.ru[:]))
        on(S.rup, n, far[BOTH], S["e%d" % s], T.eup[:], T.rup[:])
    n = len(far_tile_engs(topo, cores, s, k))
    on(S.rtc, n, d, S["e%d" % s], u8(T.ec[:, cut(s, ROWS)]), u8(T.rt[:]))
    on(S.rtp, n, d, S["e%d" % s], T.ep[:, cut(s, ROWS)], T.rtp[:])
    g.wait_ge(S.ls, sent[0])


def rank_core(g, core, T, topo, cores, r):
    S = T.sem
    near, far, rel = near_ranks(topo, cores, r), far_sorted(topo, cores, r), relays(topo, cores, r)
    hlp = helper(topo, cores, r)
    V, A, P, Y = g.vector, g.scalar, g.tensor, g.sync
    Copy = ActivationFunctionType.Copy
    add, mult, big = AluOpType.add, AluOpType.mult, AluOpType.max

    def ofs(d):
        return T.woff[:, cut(d, 32)]

    def expert(d):
        return T.wb[:].indirect(ofs(d))

    def made(d):
        return T.ws[:, cut(d, 512)]

    def part(d, q):
        a, b = (0, VPART) if q == 0 else (VPART, 32)
        return T.ws[:, 512 * d + 16 * a:512 * d + 16 * b], T.wb[:].indirect(T.woff[:, 32 * d + a:32 * d + b])

    def quantise(d, sem):
        V.quantize_mx(T.wq[:, cut(d, ROWS)], T.wp[:, cut(d, ROWS)], made(d)).then_inc(sem, 1)

    by_slot = sorted(far, key=lambda h: slot(topo, cores, h, r))
    both = by_slot[BOTH]
    order = [r, near[1], both, N, near[2], near[0]] + by_slot[:BOTH]
    last, half = order[-1], SL // 2

    for q in range(0, 4):
        Y.dma_start(T.selsrc[cut(q, 16), :], T.sel[:]).then_inc(S.lsel, 16)
    for q in range(0, 4):
        Y.dma_start(T.sendr[cut(q, 16), :], T.send[:]).then_inc(S.lsend, 16)
    for m in range(2):
        Y.dma_start(T.wb[:, cut(m, 512)], T.w[cut(m, 128), :]).then_inc(S.lw, 16)
    Y.wait_ge(S.lsel, 128)
    Y.dma_start(T.selt[:, OWN0:OWN0 + 1], T.selsrc[:]).then_inc(S.lown, 16)
    Y.dma_start(T.plr[:], T.place[:]).then_inc(S.lpo, 16)
    Y.dma_start(T.ofr[:], T.of[:]).then_inc(S.lpo, 16)
    Y.wait_ge(S.xqd, 1)
    Y.dma_start(u8(T.xc[:, cut(r, CAPP)]), u8(T.xq[:, cut(r, CAPP)])).then_inc(S.own, 16)
    Y.dma_start(T.xcp[:, cut(r, CAPP)], T.xp[:, cut(r, CAPP)]).then_inc(S.own, 16)
    Y.wait_ge(S.vp3, 1)
    for q in range(8):
        Y.dma_start(T.yoff[cut(q, 16), :], T.y16[:]).then_inc(S.lyo, 16)
    Y.wait_ge(S.yv, 1)
    Y.dma_start(T.y[:, 0:128], T.yo[:, 0:128]).then_inc(S.stv, 16)
    Y.wait_ge(S.stv, 16)

    g.iota(T.ip[:], [[0, 32]], 0, 1).then_inc(S.it, 1)
    g.iota(T.ic[:], [[16, 32]], 0, 0).then_inc(S.it, 1)
    g.wait_ge(S.lsel, 128)
    g.remote_dma_fused([RemoteDMATransfer(
        dst_ids=[dst_id(topo, core, c) for c in rel[:BOTH]], dma_engine_mask=bits(outer(topo, cores, r)[:1]),
        remote_sem=S.sela, srcs=[T.selsrc[:]], dsts=[T.rsel[:] for c in rel[:BOTH]])], local_sem=S.ls)
    sent = 1
    ts = []
    for k, d in enumerate(near):
        c = NEAR0 + near_ranks(topo, cores, d).index(r)
        e = outer(topo, cores, r)[k * NEAR_ENGS:(k + 1) * NEAR_ENGS]
        ts.append(xfer(topo, core, cores[d], e, S.seln, T.selsrc[:], T.selt[:, c:c + 1]))
        sent += len(e)
    g.remote_dma_fused(ts, local_sem=S.ls)

    g.wait_ge(S.xqd, 1)
    for plane, src, via, via2, to, sem in (
            (0, lambda d: u8(T.xq[:, cut(d, CAPP)]), u8(T.rc[:]), u8(T.rc2[:]), u8(T.xc[:, cut(r, CAPP)]), S.rcc),
            (1, lambda d: T.xp[:, cut(d, CAPP)], T.rcp[:], T.rcp2[:], T.xcp[:, cut(r, CAPP)], S.rcp)):
        ts = []
        for k, d in enumerate(far):
            e = far_col_engs(topo, cores, r, k)
            ts.append(xfer(topo, core, rel[k], e, sem, src(d), via2 if k == BOTH else via))
            sent += len(e)
        for d in near:
            e = near_col_engs(topo, cores, r, d, plane)
            ts.append(xfer(topo, core, cores[d], e, S.cx, src(d), to))
            sent += len(e)
        g.remote_dma_fused(ts, local_sem=S.ls)
    g.wait_ge(S.uqd, 1)
    e = far_tile_engs(topo, cores, r, BOTH)
    for src, via, sem in ((u8(T.uq[:]), u8(T.ru[:]), S.ruc), (T.up[:], T.rup[:], S.rup)):
        rid, pid = topo.addr(rel[BOTH], core)
        g.remote_dma(via, src, sem, S.ls, pid, rid, bits(e))
        sent += len(e)

    def tiles(dests):
        n = 0
        for src, via, to, sem, hvia, hsem in (
                (lambda d: u8(T.wq[:, cut(d, ROWS)]), u8(T.rt[:]), u8(T.ec[:, cut(r, ROWS)]), S.rtc, u8(T.ht[:]), S.htc),
                (lambda d: T.wp[:, cut(d, ROWS)], T.rtp[:], T.ep[:, cut(r, ROWS)], S.rtp, T.htp[:], S.htp)):
            ts = []
            for d in dests:
                if d in far:
                    k = far.index(d)
                    e = far_tile_engs(topo, cores, r, k)
                    ts.append(xfer(topo, core, rel[k], e, sem, src(d), via))
                else:
                    e = near_tile_engs(topo, cores, r, d)
                    ts.append(xfer(topo, core, hlp, e, hsem, src(d), hvia) if d == near[0] else
                              xfer(topo, core, cores[d], e, S["e%d" % r], src(d), to))
                n += len(e)
            g.remote_dma_fused(ts, local_sem=S.ls)
        return n

    g.wait_ge(S.hq, 2)
    sent += tiles(near[:2])
    g.wait_ge(S.bq0, 2)
    sent += tiles(far[:2])
    g.wait_ge(S.bq1, 2)
    sent += tiles(near[2:] + far[2:3])
    g.wait_ge(S.ls, sent)

    def spread(c, n, sem):
        V.tensor_copy(T.selo[:, c:c + n], T.selt[:, c:c + n]).then_inc(sem, 1)
        V.wait_ge(sem, 1)
        V.tensor_copy(T.bc[:, 16 * c:16 * (c + n)], T.two[:].indirect(T.selo[:, c:c + n])).then_inc(sem, 1)
        V.wait_ge(sem, 2)

    def aim(d, c, sem):
        V.tensor_scalar(ofs(d), T.base[:], T.bc[:, 16 * c + r:16 * c + r + 1], None, add).then_inc(sem, 1)

    V.memset(T.two[:, 0:1], 0.0).then_inc(S.two, 1)
    V.memset(T.two[:, 1:2], 512.0).then_inc(S.two, 1)
    V.wait_ge(S.it, 2)
    V.tensor_scalar(T.pm[:], T.ip[:], 15, None, AluOpType.bitwise_and).then_inc(S.vb, 1)
    V.wait_ge(S.vb, 1)
    V.tensor_tensor(T.base[:], T.pm[:], T.ic[:], add).then_inc(S.vb, 1)
    V.wait_ge(S.lsend, 128)
    V.tensor_scalar(T.xoff[:], T.sendr[:], 0.0, 4.0, big, mult).then_inc(S.vx, 1)
    V.wait_ge(S.vx, 1)
    V.wait_ge(S.lx, 16)
    for t in (0, 1):
        V.tensor_copy(T.xs[:, t:4 * SL:4], T.xb[:, t:4 * COLS].indirect(T.xoff[:])).then_inc(S.xg, 1)
    V.wait_ge(S.lw, 32)
    V.quantize_mx(T.uq[:], T.up[:], T.wb[:]).then_inc(S.uqd, 1)
    V.wait_ge(S.xg, 2)
    V.wait_ge(S.xgs, 2)
    V.quantize_mx(T.xq[:], T.xp[:], T.xs[:]).then_inc(S.xqd, 1)
    V.wait_ge(S.vb, 2)
    V.wait_ge(S.two, 2)
    V.wait_ge(S.lown, 16)
    spread(OWN0, 1, S.vown)
    aim(r, OWN0, S.vown)
    V.wait_ge(S.lpo, 32)
    c = 16 * OWN0 + both
    V.tensor_scalar(T.ofm[:], T.ofr[:], float(SL), None, mult).then_inc(S.vp1, 1)
    V.tensor_scalar(T.ofu[:], T.ofr[:], float(both), T.bc[0:16, c:c + 1], AluOpType.is_equal, mult).then_inc(S.vp1, 1)
    V.wait_ge(S.vp1, 2)
    V.tensor_tensor(T.ysum[:], T.ofm[:], T.plr[:], add).then_inc(S.vp2, 1)
    V.tensor_scalar(T.ofv[:], T.ofu[:], (N - both) * SL / 512.0, None, mult).then_inc(S.vp2, 1)
    V.wait_ge(S.vp2, 2)
    V.tensor_tensor(T.yall[:], T.ysum[:], T.ofv[:], add).then_inc(S.vp4, 1)
    V.wait_ge(S.vp4, 1)
    V.tensor_copy(T.y16[:], T.yall[:]).then_inc(S.vp3, 1)
    V.wait_ge(S.seln, NEAR_ENGS * len(near))
    spread(NEAR0, len(near), S.von)
    for i, d in enumerate(near):
        aim(d, NEAR0 + i, S.voa)
    V.wait_ge(S.voa, len(near))
    V.tensor_copy(made(near[0]), expert(near[0])).then_inc(S.vga, 1)
    V.wait_ge(S.vga, 1)
    quantise(near[0], S.hq)
    V.wait_ge(S.sgo, 1)
    V.quantize_mx(T.ec[:, cut(r, ROWS)], T.ep[:, cut(r, ROWS)], made(r)).then_inc(S.oq, 1)
    V.wait_ge(S.sga0, 1)
    quantise(near[1], S.hq)
    V.wait_ge(S.selx, SEL_ENGS * BOTH)
    spread(FAR0, BOTH, S.vbf)
    for d in far[:2]:
        aim(d, FAR0 + far.index(d), S.vob0)
    V.wait_ge(S.vob0, 2)
    V.tensor_copy(made(far[0]), expert(far[0])).then_inc(S.vb0, 1)
    aim(far[2], FAR0 + 2, S.vob1)
    V.wait_ge(S.vb0, 1)
    quantise(far[0], S.bq0)
    V.wait_ge(S.sb0, 1)
    quantise(far[1], S.bq0)
    V.wait_ge(S.vob1, 1)
    V.tensor_copy(*part(far[2], 0)).then_inc(S.vb1, 1)
    V.wait_ge(S.sga1, 1)
    quantise(near[2], S.bq1)
    V.wait_ge(S.vb1, 1)
    V.wait_ge(S.sb1, 1)
    quantise(far[2], S.bq1)

    def bank(i):
        return 512 * i

    def block(i):
        return cut(order[i], SL)

    for i in range(0, N, 2):
        V.wait_ge(S["m%d" % i], 1)
        V.tensor_copy(T.res[:, block(i)], T.ps[:, bank(i):bank(i) + SL]).then_inc(S.c0 if i == 0 else S.cv, 1)
    V.wait_ge(S.m8, 2)
    V.tensor_copy(T.res[:, SL * last:SL * last + half], T.ps[:, 0:half]).then_inc(S.cv, 1)
    V.wait_ge(S.lyo, 128)
    V.wait_ge(S.c0, 1)
    V.wait_ge(S.c1, 1)
    V.wait_ge(S.cv, 4)
    V.wait_ge(S.cs, 4)
    V.tensor_copy(T.yo[:, 0:128], T.res[:].indirect(T.yoff[:, 0:8])).then_inc(S.yv, 1)

    for q in range(4, 8):
        A.dma_start(T.selsrc[cut(q, 16), :], T.sel[:]).then_inc(S.lsel, 16)
    for q in range(4, 8):
        A.dma_start(T.sendr[cut(q, 16), :], T.send[:]).then_inc(S.lsend, 16)
    A.dma_start(T.xb[:], T.x[:]).then_inc(S.lx, 16)
    A.wait_ge(S.vx, 1)
    A.wait_ge(S.lx, 16)
    for t in (2, 3):
        A.activation(T.xs[:, t:4 * SL:4], T.xb[:, t:4 * COLS].indirect(T.xoff[:]), Copy).then_inc(S.xgs, 1)
    A.wait_ge(S.lw, 32)
    A.wait_ge(S.vown, 3)
    A.activation(made(r), expert(r), Copy).then_inc(S.sgo, 1)
    A.wait_ge(S.voa, len(near))
    for i, d in enumerate(near[1:]):
        A.activation(made(d), expert(d), Copy).then_inc(S["sga%d" % i], 1)
    A.wait_ge(S.vob0, 2)
    A.activation(made(far[1]), expert(far[1]), Copy).then_inc(S.sb0, 1)
    A.wait_ge(S.vob1, 1)
    A.activation(*part(far[2], 1), Copy).then_inc(S.sb1, 1)
    for i in range(1, N, 2):
        A.wait_ge(S["m%d" % i], 1)
        A.activation(T.res[:, block(i)], T.ps[:, bank(i):bank(i) + SL], Copy).then_inc(S.c1 if i == 1 else S.cs, 1)
    A.wait_ge(S.m8, 2)
    A.activation(T.res[:, SL * last + half:SL * (last + 1)], T.ps[:, 512:512 + half], Copy).then_inc(S.cs, 1)
    A.wait_ge(S.lyo, 128)
    A.wait_ge(S.cs, 4)
    A.wait_ge(S.c1, 1)
    A.wait_ge(S.c0, 1)
    A.wait_ge(S.cv, 4)
    A.activation(T.yo[:, 128:256], T.res[:].indirect(T.yoff[:, 8:16]), Copy).then_inc(S.ys, 1)
    A.wait_ge(S.ys, 1)
    A.dma_start(T.y[:, 128:256], T.yo[:, 128:256]).then_inc(S.sts, 16)
    A.wait_ge(S.sts, 16)

    P.wait_ge(S.own, 32)
    P.wait_ge(S.cx, sum(landed(topo, cores, s, r, False) for s in near + far))
    for i, h in enumerate(order):
        if h in (both, N):
            m = int(h == N)
            w, p = T.eu[:, cut(m, ROWS)], T.eup[:, cut(m, ROWS)]
            P.wait_ge(S["e%d" % both], landed(topo, cores, both, r, True))
        else:
            w, p = T.ec[:, cut(h, ROWS)], T.ep[:, cut(h, ROWS)]
            P.wait_ge(S.oq if h == r else S["e%d" % h], 1 if h == r else landed(topo, cores, h, r, True))
        if i < N:
            P.matmul_mx(T.ps[:, bank(i):bank(i) + SL], w, p, T.xc[:], T.xcp[:], True, True).then_inc(S["m%d" % i], 1)
        else:
            P.wait_ge(S.c0, 1)
            P.matmul_mx(T.ps[:, 0:half], w, p, T.xc[:, 0:half], T.xcp[:, 0:half], True, True).then_inc(S.m8, 1)
            P.wait_ge(S.c1, 1)
            P.matmul_mx(T.ps[:, 512:512 + half], w, p, T.xc[:, half:SL], T.xcp[:, half:SL], True, True).then_inc(S.m8, 1)
